import numpy as np
import ml_dtypes


def mxq(x, axis, fmt="e4m3"):
    dtype, down = {"e4m3": (ml_dtypes.float8_e4m3fn, 7), "e5m2": (ml_dtypes.float8_e5m2, 14)}[fmt]
    v = np.moveaxis(np.asarray(x, np.float32).astype(ml_dtypes.bfloat16).astype(np.float64), axis, -1)
    blocks = v.reshape(v.shape[:-1] + (-1, 32))
    amax = np.abs(blocks).max(-1, keepdims=True)
    byte = np.maximum(np.where(amax > 0, np.frexp(amax)[1] - 1 + 127, 0) - down, 1)
    scale = np.exp2(byte - 127.0)
    codes = (blocks / scale).astype(np.float32).astype(dtype).astype(np.float64)
    return np.moveaxis((codes * scale).reshape(v.shape), -1, axis)


WIDE = False


def mx_kscale(k):
    if not WIDE:
        return np.ones(k)
    levels = np.array([10, -10, 5, -5, 0])
    if k % 512:
        return np.exp2(np.random.permutation(np.resize(levels, k // 32))).repeat(32)
    a = np.empty((k // 512, 16))
    for p in range(k // 512):
        a[p, :8] = np.random.permutation(np.resize(levels, 8))
        for g in range(8):
            far = levels[np.abs(levels - a[p, g]) >= 10]
            a[p, g + 8] = far[np.random.randint(len(far))]
    return np.exp2(a.ravel()).repeat(32)


def f64(x):
    return np.asarray(x).astype(np.float64)


def striped(idx):
    return np.tile(np.asarray(idx).reshape(-1, 16).T, (8, 1)).astype(np.uint16)


def unstriped(offs):
    return offs[:16].T.reshape(-1).astype(np.int64)


E2M1 = np.array([0.0, 0.5, 1.0, 1.5, 2.0, 3.0, 4.0, 6.0, -0.0, -0.5, -1.0, -1.5, -2.0, -3.0, -4.0, -6.0])


def pack_weight(w, fmt):
    k, n = w.shape
    w = f64(np.asarray(w, np.float32).astype(ml_dtypes.bfloat16)).reshape(k // 32, 32, n)
    amax = np.abs(w).max(1)
    if fmt == "e4m3":
        byte = np.frexp(amax)[1] - 1 + 127 - 7
    else:
        mant, ex = np.frexp(amax / 6.0)
        byte = np.where(mant > 0.5, ex, ex - 1) + 127
    byte = np.clip(np.where(amax > 0, byte, 1), 1, 254)
    scaled = (w * np.exp2(127.0 - byte)[:, None, :]).reshape(k, n).astype(np.float32)
    by_word = np.ascontiguousarray(scaled.reshape(k // 512, 128, 4, n).transpose(0, 1, 3, 2))
    if fmt == "e4m3":
        words = by_word.astype(ml_dtypes.float8_e4m3fn).view(np.uint8)
    else:
        c = by_word.astype(ml_dtypes.float4_e2m1fn).view(np.uint8) & 0xF
        words = (c[..., 0::2] | (c[..., 1::2] << 4)).reshape(k // 512, 128, 2 * n)
    return np.ascontiguousarray(words), np.ascontiguousarray(byte.astype(np.uint8).reshape(k // 512, 16, n))


def unpack_weight(words, scales, fmt):
    g, _, n = scales.shape
    words = np.ascontiguousarray(words).reshape(g, 128, n, -1)
    if fmt == "e4m3":
        vals = words.view(ml_dtypes.float8_e4m3fn).astype(np.float64)
    else:
        nib = np.empty((g, 128, n, 4), np.uint8)
        nib[..., 0::2] = words & 0xF
        nib[..., 1::2] = words >> 4
        vals = E2M1[nib]
    vals = vals * np.repeat(np.exp2(scales.astype(np.float64) - 127.0), 8, axis=1)[..., None]
    return vals.transpose(0, 1, 3, 2).reshape(g * 512, n)


K, R, F, T, J, M = 512, 128, 512, 2048, 512, 256


def setup_inputs():
    n = np.random.standard_normal
    idx = np.random.permutation(T)[:J]
    idx2 = np.random.permutation(J)[:M]
    idx3 = np.random.permutation(J)[:M]
    fk = mx_kscale(K)
    dtabp = pack_weight(n((K, T)) / fk[:, None], "e2m1")
    tabp = pack_weight(n((K, T)) / fk[:, None], "e2m1")
    return {
        "dtab_words": dtabp[0],
        "dtab_scales": dtabp[1],
        "tab_words": tabp[0],
        "tab_scales": tabp[1],
        "w1": (n((K, R)) * 1 / np.sqrt(K) * fk[:, None]).astype(np.float32),
        "reserve": (np.random.uniform(0.3, 1.5, (R, 1))).astype(np.float32),
        "og": (np.random.uniform(0.5, 2.0, (R, 1))).astype(np.float32),
        "base": (0.3 * n((R, M))).astype(np.float32),
        "offs": striped(idx),
        "offs2": striped(idx2),
        "offs3": striped(idx3),
    }


def reference(dtab_words, dtab_scales, tab_words, tab_scales, w1, reserve, og, base, offs, offs2, offs3):
    idx = unstriped(offs)
    idx2 = unstriped(offs2)
    idx3 = unstriped(offs3)
    dtabu = unpack_weight(dtab_words, dtab_scales, "e2m1")
    tabu = unpack_weight(tab_words, tab_scales, "e2m1")
    w1q = mxq(f64(w1), 0, "e4m3")
    tabidxg = tabu[:, idx]
    a = w1q.T @ tabidxg
    dtabidxg = dtabu[:, idx]
    ta = w1q.T @ dtabidxg
    h1 = np.exp(a)
    th1 = ta * h1
    tu1 = (th1[:, idx2] - (th1[:, idx2] + th1[:, idx3]) * h1[:, idx2] / (h1[:, idx2] + h1[:, idx3] + f64(reserve))) / (h1[:, idx2] + h1[:, idx3] + f64(reserve))
    y = tu1 * f64(og) + f64(base)
    return y

@@ -1,0 +1,123 @@
+from contextlib import ExitStack
+
+import concourse.mybir as mybir
+
+K, R, T, J, M = 512, 128, 2048, 512, 256
+FLOPS = 2 * 2 * K * R * J
+
+F32 = mybir.dt.float32
+BF16 = mybir.dt.bfloat16
+I32 = mybir.dt.int32
+U32 = mybir.dt.uint32
+U16 = mybir.dt.uint16
+U8 = mybir.dt.uint8
+FP8X4 = mybir.dt.float8_e4m3fn_x4
+FP4X4 = mybir.dt.float4_e2m1fn_x4
+ACT = mybir.ActivationFunctionType
+ALU = mybir.AluOpType
+
+P = 128
+HALVES = 2
+
+
+def tile_attend_tratiopairs_kernel(tc, dtab_words, dtab_scales, tab_words, tab_scales, w1, reserve, og, base, offs, offs2, offs3, out):
+    nc = tc.nc
+    with ExitStack() as ctx:
+        sb = ctx.enter_context(tc.tile_pool(name="sb", bufs=1))
+        ps = ctx.enter_context(tc.psum_pool(name="ps", bufs=1))
+
+        list1 = sb.tile([P, J // 16], U16, name="list1")
+        list2 = sb.tile([P, M // 16], U16, name="list2")
+        list3 = sb.tile([P, M // 16], U16, name="list3")
+        tw = sb.tile([P, T], U16, name="tw", tag="tw", align_bytes=64)
+        ts = sb.tile([P, T], U8, name="ts", tag="ts", align_bytes=64)
+        ds = sb.tile([P, T], U8, name="ds", tag="ds", align_bytes=64)
+        w_raw = sb.tile([P, 4, R], F32, name="w_raw", tag="w_raw", align_bytes=64)
+
+        def load_scales(engine, plane, src):
+            rows = src[0].bitcast(I32).rearrange("(q r) c -> r q c", r=4)
+            for r in range(4):
+                engine.dma_start(out=plane[r:P:32, :].bitcast(I32), in_=rows[r])
+
+        nc.vector.memset(ts[:].bitcast(U32), 0)
+        nc.vector.memset(ds[:].bitcast(U32), 0)
+        nc.sync.dma_start(list1[:], offs)
+        nc.scalar.dma_start(out=tw[:].bitcast(I32), in_=tab_words[0].bitcast(I32))
+        nc.scalar.dma_start(out=w_raw[:], in_=w1.rearrange("(p t) r -> p t r", t=4))
+        load_scales(nc.sync, ts, tab_scales)
+        nc.sync.dma_start(list2[:], offs2)
+        nc.sync.dma_start(list3[:], offs3)
+        load_scales(nc.sync, ds, dtab_scales)
+
+        w_bf = sb.tile([P, R, 4], BF16, name="w_bf", tag="w_bf", align_bytes=64)
+        nc.scalar.activation(w_bf[:], w_raw[:].rearrange("p t r -> p r t"), ACT.Copy)
+        dw = sb.tile([P, T], U16, name="dw", tag="w_raw", align_bytes=64)
+        nc.scalar.dma_start(out=dw[:].bitcast(I32), in_=dtab_words[0].bitcast(I32))
+        w_codes = sb.tile([P, R], U32, name="w_codes", align_bytes=64)
+        w_scales = sb.tile([P, R], U8, name="w_scales", align_bytes=64)
+
+        tw_g = sb.tile([P, J], U16, name="tw_g", align_bytes=64)
+        ts_g = sb.tile([P, J], U8, name="ts_g", align_bytes=64)
+        ds_g = sb.tile([P, J], U8, name="ds_g", align_bytes=64)
+
+        nc.vector.tensor_copy(tw_g[:], tw[:].indirect(list1[:]))
+        nc.vector.tensor_copy(ts_g[:], ts[:].indirect(list1[:]))
+        nc.vector.quantize_mx(out=w_codes[:].bitcast(FP8X4), scales=w_scales[:], in_=w_bf[:].rearrange("p r t -> p (r t)"))
+
+        a_ps = ps.tile([P, J], F32, name="a_ps")
+        nc.tensor.matmul_mx(out=a_ps[:], lhsT=w_codes[:].bitcast(FP8X4), lhsT_scale=w_scales[:],
+                            rhs=tw_g[:].bitcast(FP4X4), rhs_scale=ts_g[:], start=True, stop=True)
+        h1 = sb.tile([P, J], F32, name="h1")
+        nc.scalar.activation(h1[:], a_ps[:], ACT.Exp)
+
+        res_t = sb.tile([P, 1], F32, name="res_t", tag="tw", align_bytes=64)
+        nc.sync.dma_start(out=res_t[:], in_=reserve)
+        base_t = sb.tile([P, M], F32, name="base_t", tag="ts", align_bytes=64)
+        nc.sync.dma_start(out=base_t[:], in_=base)
+        og_t = sb.tile([P, 1], F32, name="og_t", tag="w_bf", align_bytes=64)
+        nc.sync.dma_start(out=og_t[:], in_=og)
+
+        nc.vector.tensor_copy(ds_g[:], ds[:].indirect(list1[:]))
+        ta_ps = ps.tile([P, J], F32, name="ta_ps")
+        JH = J // 2
+        for i in range(2):
+            dw_g = sb.tile([P, JH], U16, name="dw_g%d" % i, tag="dw_g%d" % i, align_bytes=64)
+            nc.vector.tensor_copy(dw_g[:], dw[:].indirect(list1[:, i * JH // 16:(i + 1) * JH // 16]))
+            nc.tensor.matmul_mx(out=ta_ps[:, i * JH:(i + 1) * JH], lhsT=w_codes[:].bitcast(FP8X4), lhsT_scale=w_scales[:],
+                                rhs=dw_g[:].bitcast(FP4X4), rhs_scale=ds_g[:, i * JH:(i + 1) * JH], start=True, stop=True)
+
+        h_2 = sb.tile([P, M], F32, name="h_2", tag="dw_g0", align_bytes=64)
+        h_3 = sb.tile([P, M], F32, name="h_3", tag="ds", align_bytes=64)
+        nc.vector.tensor_copy(h_2[:], h1[:].indirect(list2[:]))
+        nc.vector.tensor_copy(h_3[:], h1[:].indirect(list3[:]))
+        th1 = sb.tile([P, J], F32, name="th1")
+        nc.vector.tensor_tensor(th1[:], ta_ps[:], h1[:], ALU.mult)
+
+        W = M // HALVES
+        cols = [slice(i * W, (i + 1) * W) for i in range(HALVES)]
+        ents = [slice(i * W // 16, (i + 1) * W // 16) for i in range(HALVES)]
+
+        def part(name):
+            return [sb.tile([P, W], F32, name="%s%d" % (name, i)) for i in range(HALVES)]
+
+        pair, root, inv, inv2 = part("pair"), part("root"), part("inv"), part("inv2")
+        y, x, u, v, o = part("y"), part("x"), part("u"), part("v"), part("o")
+        for i in range(HALVES):
+            nc.vector.tensor_tensor(pair[i][:], h_2[:, cols[i]], h_3[:, cols[i]], ALU.add)
+        for i in range(HALVES):
+            nc.scalar.activation(root[i][:], pair[i][:], ACT.Abs_reciprocal_sqrt, bias=res_t[:])
+            nc.scalar.activation(pair[i][:], h_3[:, cols[i]], ACT.Identity, bias=res_t[:])
+        for i in range(HALVES):
+            nc.scalar.activation(inv[i][:], root[i][:], ACT.Square)
+            nc.scalar.activation(inv2[i][:], inv[i][:], ACT.Square)
+        for i in range(HALVES):
+            nc.vector.tensor_tensor(y[i][:], th1[:].indirect(list3[:, ents[i]]), h_2[:, cols[i]], ALU.mult)
+        for i in range(HALVES):
+            nc.vector.tensor_tensor(x[i][:], th1[:].indirect(list2[:, ents[i]]), pair[i][:], ALU.mult)
+        for i in range(HALVES):
+            nc.vector.tensor_tensor(u[i][:], x[i][:], y[i][:], ALU.subtract)
+        for i in range(HALVES):
+            nc.vector.scalar_tensor_tensor(v[i][:], u[i][:], og_t[:], inv2[i][:], ALU.mult, ALU.mult)
+        for i in range(HALVES):
+            nc.vector.tensor_tensor(o[i][:], v[i][:], base_t[:, cols[i]], ALU.add)
+            nc.sync.dma_start(out=out[:, cols[i]], in_=o[i][:])

@@ -31,6 +31,7 @@ def tile_attend_tratiopairs_kernel(tc, dtab_words, dtab_scales, tab_words, tab_s
         list3 = sb.tile([P, M // 16], U16, name="list3")
         tw = sb.tile([P, T], U16, name="tw", tag="tw", align_bytes=64)
         ts = sb.tile([P, T], U8, name="ts", tag="ts", align_bytes=64)
+        dw = sb.tile([P, T], U16, name="dw", align_bytes=64)
         ds = sb.tile([P, T], U8, name="ds", tag="ds", align_bytes=64)
         w_raw = sb.tile([P, 4, R], F32, name="w_raw", tag="w_raw", align_bytes=64)
 
@@ -41,55 +42,52 @@ def tile_attend_tratiopairs_kernel(tc, dtab_words, dtab_scales, tab_words, tab_s
 
         nc.vector.memset(ts[:].bitcast(U32), 0)
         nc.vector.memset(ds[:].bitcast(U32), 0)
+        nc.sync.dma_start(out=tw[:].bitcast(I32), in_=tab_words[0].bitcast(I32))
         nc.sync.dma_start(list1[:], offs)
-        nc.scalar.dma_start(out=tw[:].bitcast(I32), in_=tab_words[0].bitcast(I32))
-        nc.scalar.dma_start(out=w_raw[:], in_=w1.rearrange("(p t) r -> p t r", t=4))
-        load_scales(nc.sync, ts, tab_scales)
         nc.sync.dma_start(list2[:], offs2)
-        nc.sync.dma_start(list3[:], offs3)
+        load_scales(nc.sync, ts, tab_scales)
+        nc.sync.dma_start(out=w_raw[:], in_=w1.rearrange("(p t) r -> p t r", t=4))
         load_scales(nc.sync, ds, dtab_scales)
+        nc.sync.dma_start(out=dw[:].bitcast(I32), in_=dtab_words[0].bitcast(I32))
+        nc.sync.dma_start(list3[:], offs3)
 
         w_bf = sb.tile([P, R, 4], BF16, name="w_bf", tag="w_bf", align_bytes=64)
         nc.scalar.activation(w_bf[:], w_raw[:].rearrange("p t r -> p r t"), ACT.Copy)
-        dw = sb.tile([P, T], U16, name="dw", tag="w_raw", align_bytes=64)
-        nc.scalar.dma_start(out=dw[:].bitcast(I32), in_=dtab_words[0].bitcast(I32))
         w_codes = sb.tile([P, R], U32, name="w_codes", align_bytes=64)
-        w_scales = sb.tile([P, R], U8, name="w_scales", align_bytes=64)
 
         tw_g = sb.tile([P, J], U16, name="tw_g", align_bytes=64)
         ts_g = sb.tile([P, J], U8, name="ts_g", align_bytes=64)
-        ds_g = sb.tile([P, J], U8, name="ds_g", align_bytes=64)
 
         nc.vector.tensor_copy(tw_g[:], tw[:].indirect(list1[:]))
         nc.vector.tensor_copy(ts_g[:], ts[:].indirect(list1[:]))
+        w_scales = sb.tile([P, R], U8, name="w_scales", align_bytes=64)
         nc.vector.quantize_mx(out=w_codes[:].bitcast(FP8X4), scales=w_scales[:], in_=w_bf[:].rearrange("p r t -> p (r t)"))
 
         a_ps = ps.tile([P, J], F32, name="a_ps")
         nc.tensor.matmul_mx(out=a_ps[:], lhsT=w_codes[:].bitcast(FP8X4), lhsT_scale=w_scales[:],
                             rhs=tw_g[:].bitcast(FP4X4), rhs_scale=ts_g[:], start=True, stop=True)
-        h1 = sb.tile([P, J], F32, name="h1")
-        nc.scalar.activation(h1[:], a_ps[:], ACT.Exp)
 
         res_t = sb.tile([P, 1], F32, name="res_t", tag="tw", align_bytes=64)
         nc.sync.dma_start(out=res_t[:], in_=reserve)
-        base_t = sb.tile([P, M], F32, name="base_t", tag="ts", align_bytes=64)
+        base_t = sb.tile([P, M], F32, name="base_t", tag="w_raw", align_bytes=64)
         nc.sync.dma_start(out=base_t[:], in_=base)
         og_t = sb.tile([P, 1], F32, name="og_t", tag="w_bf", align_bytes=64)
         nc.sync.dma_start(out=og_t[:], in_=og)
 
+        dw_g = sb.tile([P, J], U16, name="dw_g", tag="dw_g", align_bytes=64)
+        ds_g = sb.tile([P, J], U8, name="ds_g", tag="ds_g", align_bytes=64)
         nc.vector.tensor_copy(ds_g[:], ds[:].indirect(list1[:]))
+        h1 = sb.tile([P, J], F32, name="h1", tag="ds", align_bytes=64)
+        nc.scalar.activation(h1[:], a_ps[:], ACT.Exp)
+        nc.vector.tensor_copy(dw_g[:], dw[:].indirect(list1[:]))
         ta_ps = ps.tile([P, J], F32, name="ta_ps")
-        JH = J // 2
-        for i in range(2):
-            dw_g = sb.tile([P, JH], U16, name="dw_g%d" % i, tag="dw_g%d" % i, align_bytes=64)
-            nc.vector.tensor_copy(dw_g[:], dw[:].indirect(list1[:, i * JH // 16:(i + 1) * JH // 16]))
-            nc.tensor.matmul_mx(out=ta_ps[:, i * JH:(i + 1) * JH], lhsT=w_codes[:].bitcast(FP8X4), lhsT_scale=w_scales[:],
-                                rhs=dw_g[:].bitcast(FP4X4), rhs_scale=ds_g[:, i * JH:(i + 1) * JH], start=True, stop=True)
+        nc.tensor.matmul_mx(out=ta_ps[:], lhsT=w_codes[:].bitcast(FP8X4), lhsT_scale=w_scales[:],
+                            rhs=dw_g[:].bitcast(FP4X4), rhs_scale=ds_g[:], start=True, stop=True)
 
-        h_2 = sb.tile([P, M], F32, name="h_2", tag="dw_g0", align_bytes=64)
-        h_3 = sb.tile([P, M], F32, name="h_3", tag="ds", align_bytes=64)
-        nc.vector.tensor_copy(h_2[:], h1[:].indirect(list2[:]))
-        nc.vector.tensor_copy(h_3[:], h1[:].indirect(list3[:]))
+        h_23 = sb.tile([P, 2, M], F32, name="h_23")
+        h_2, h_3 = h_23[:, 0, :], h_23[:, 1, :]
+        nc.vector.tensor_copy(h_2, h1[:].indirect(list2[:]))
+        nc.vector.tensor_copy(h_3, h1[:].indirect(list3[:]))
         th1 = sb.tile([P, J], F32, name="th1")
         nc.vector.tensor_tensor(th1[:], ta_ps[:], h1[:], ALU.mult)
 
@@ -100,7 +98,8 @@ def tile_attend_tratiopairs_kernel(tc, dtab_words, dtab_scales, tab_words, tab_s
         def part(name):
             return [sb.tile([P, W], F32, name="%s%d" % (name, i)) for i in range(HALVES)]
 
-        pair, root, inv, inv2 = part("pair"), part("root"), part("inv"), part("inv2")
+        pair = [sb.tile([P, W], F32, name="pair%d" % i, tag=("dw_g", "ds_g")[i], align_bytes=64) for i in range(HALVES)]
+        root, inv, inv2 = part("root"), part("inv"), part("inv2")
         y, x, u, v, o = part("y"), part("x"), part("u"), part("v"), part("o")
         for i in range(HALVES):
             nc.vector.tensor_tensor(pair[i][:], h_2[:, cols[i]], h_3[:, cols[i]], ALU.add)

from contextlib import ExitStack

import concourse.mybir as mybir

K, R, T, J, M = 512, 128, 2048, 512, 256
FLOPS = 2 * 2 * K * R * J

F32 = mybir.dt.float32
BF16 = mybir.dt.bfloat16
I32 = mybir.dt.int32
U32 = mybir.dt.uint32
U16 = mybir.dt.uint16
U8 = mybir.dt.uint8
FP8X4 = mybir.dt.float8_e4m3fn_x4
FP4X4 = mybir.dt.float4_e2m1fn_x4
ACT = mybir.ActivationFunctionType
ALU = mybir.AluOpType

P = 128
HALVES = 2


def tile_attend_tratiopairs_kernel(tc, dtab_words, dtab_scales, tab_words, tab_scales, w1, reserve, og, base, offs, offs2, offs3, out):
    nc = tc.nc
    with ExitStack() as ctx:
        sb = ctx.enter_context(tc.tile_pool(name="sb", bufs=1))
        ps = ctx.enter_context(tc.psum_pool(name="ps", bufs=1))

        list1 = sb.tile([P, J // 16], U16, name="list1")
        list2 = sb.tile([P, M // 16], U16, name="list2")
        list3 = sb.tile([P, M // 16], U16, name="list3")
        tw = sb.tile([P, T], U16, name="tw", tag="tw", align_bytes=64)
        ts = sb.tile([P, T], U8, name="ts", tag="ts", align_bytes=64)
        dw = sb.tile([P, T], U16, name="dw", align_bytes=64)
        ds = sb.tile([P, T], U8, name="ds", tag="ds", align_bytes=64)
        w_raw = sb.tile([P, 4, R], F32, name="w_raw", tag="w_raw", align_bytes=64)

        def load_scales(engine, plane, src):
            rows = src[0].bitcast(I32).rearrange("(q r) c -> r q c", r=4)
            for r in range(4):
                engine.dma_start(out=plane[r:P:32, :].bitcast(I32), in_=rows[r])

        nc.vector.memset(ts[:].bitcast(U32), 0)
        nc.vector.memset(ds[:].bitcast(U32), 0)
        nc.sync.dma_start(out=tw[:].bitcast(I32), in_=tab_words[0].bitcast(I32))
        nc.sync.dma_start(list1[:], offs)
        nc.sync.dma_start(list2[:], offs2)
        load_scales(nc.sync, ts, tab_scales)
        nc.sync.dma_start(out=w_raw[:], in_=w1.rearrange("(p t) r -> p t r", t=4))
        load_scales(nc.sync, ds, dtab_scales)
        nc.sync.dma_start(out=dw[:].bitcast(I32), in_=dtab_words[0].bitcast(I32))
        nc.sync.dma_start(list3[:], offs3)

        w_bf = sb.tile([P, R, 4], BF16, name="w_bf", tag="w_bf", align_bytes=64)
        nc.scalar.activation(w_bf[:], w_raw[:].rearrange("p t r -> p r t"), ACT.Copy)
        w_codes = sb.tile([P, R], U32, name="w_codes", align_bytes=64)

        tw_g = sb.tile([P, J], U16, name="tw_g", align_bytes=64)
        ts_g = sb.tile([P, J], U8, name="ts_g", align_bytes=64)

        nc.vector.tensor_copy(tw_g[:], tw[:].indirect(list1[:]))
        nc.vector.tensor_copy(ts_g[:], ts[:].indirect(list1[:]))
        w_scales = sb.tile([P, R], U8, name="w_scales", align_bytes=64)
        nc.vector.quantize_mx(out=w_codes[:].bitcast(FP8X4), scales=w_scales[:], in_=w_bf[:].rearrange("p r t -> p (r t)"))

        a_ps = ps.tile([P, J], F32, name="a_ps")
        nc.tensor.matmul_mx(out=a_ps[:], lhsT=w_codes[:].bitcast(FP8X4), lhsT_scale=w_scales[:],
                            rhs=tw_g[:].bitcast(FP4X4), rhs_scale=ts_g[:], start=True, stop=True)

        res_t = sb.tile([P, 1], F32, name="res_t", tag="tw", align_bytes=64)
        nc.sync.dma_start(out=res_t[:], in_=reserve)
        base_t = sb.tile([P, M], F32, name="base_t", tag="w_raw", align_bytes=64)
        nc.sync.dma_start(out=base_t[:], in_=base)
        og_t = sb.tile([P, 1], F32, name="og_t", tag="w_bf", align_bytes=64)
        nc.sync.dma_start(out=og_t[:], in_=og)

        dw_g = sb.tile([P, J], U16, name="dw_g", tag="dw_g", align_bytes=64)
        ds_g = sb.tile([P, J], U8, name="ds_g", tag="ds_g", align_bytes=64)
        nc.vector.tensor_copy(ds_g[:], ds[:].indirect(list1[:]))
        h1 = sb.tile([P, J], F32, name="h1", tag="ds", align_bytes=64)
        nc.scalar.activation(h1[:], a_ps[:], ACT.Exp)
        nc.vector.tensor_copy(dw_g[:], dw[:].indirect(list1[:]))
        ta_ps = ps.tile([P, J], F32, name="ta_ps")
        nc.tensor.matmul_mx(out=ta_ps[:], lhsT=w_codes[:].bitcast(FP8X4), lhsT_scale=w_scales[:],
                            rhs=dw_g[:].bitcast(FP4X4), rhs_scale=ds_g[:], start=True, stop=True)

        h_23 = sb.tile([P, 2, M], F32, name="h_23")
        h_2, h_3 = h_23[:, 0, :], h_23[:, 1, :]
        nc.vector.tensor_copy(h_2, h1[:].indirect(list2[:]))
        nc.vector.tensor_copy(h_3, h1[:].indirect(list3[:]))
        th1 = sb.tile([P, J], F32, name="th1")
        nc.vector.tensor_tensor(th1[:], ta_ps[:], h1[:], ALU.mult)

        W = M // HALVES
        cols = [slice(i * W, (i + 1) * W) for i in range(HALVES)]
        ents = [slice(i * W // 16, (i + 1) * W // 16) for i in range(HALVES)]

        def part(name):
            return [sb.tile([P, W], F32, name="%s%d" % (name, i)) for i in range(HALVES)]

        pair = [sb.tile([P, W], F32, name="pair%d" % i, tag=("dw_g", "ds_g")[i], align_bytes=64) for i in range(HALVES)]
        root, inv, inv2 = part("root"), part("inv"), part("inv2")
        y, x, u, v, o = part("y"), part("x"), part("u"), part("v"), part("o")
        for i in range(HALVES):
            nc.vector.tensor_tensor(pair[i][:], h_2[:, cols[i]], h_3[:, cols[i]], ALU.add)
        for i in range(HALVES):
            nc.scalar.activation(root[i][:], pair[i][:], ACT.Abs_reciprocal_sqrt, bias=res_t[:])
            nc.scalar.activation(pair[i][:], h_3[:, cols[i]], ACT.Identity, bias=res_t[:])
        for i in range(HALVES):
            nc.scalar.activation(inv[i][:], root[i][:], ACT.Square)
            nc.scalar.activation(inv2[i][:], inv[i][:], ACT.Square)
        for i in range(HALVES):
            nc.vector.tensor_tensor(y[i][:], th1[:].indirect(list3[:, ents[i]]), h_2[:, cols[i]], ALU.mult)
        for i in range(HALVES):
            nc.vector.tensor_tensor(x[i][:], th1[:].indirect(list2[:, ents[i]]), pair[i][:], ALU.mult)
        for i in range(HALVES):
            nc.vector.tensor_tensor(u[i][:], x[i][:], y[i][:], ALU.subtract)
        for i in range(HALVES):
            nc.vector.scalar_tensor_tensor(v[i][:], u[i][:], og_t[:], inv2[i][:], ALU.mult, ALU.mult)
        for i in range(HALVES):
            nc.vector.tensor_tensor(o[i][:], v[i][:], base_t[:, cols[i]], ALU.add)
            nc.sync.dma_start(out=out[:, cols[i]], in_=o[i][:])
